import numpy as np
import ml_dtypes


def mxq(x, axis, fmt="e4m3"):
    dtype, down = {"e4m3": (ml_dtypes.float8_e4m3fn, 7), "e5m2": (ml_dtypes.float8_e5m2, 14)}[fmt]
    v = np.moveaxis(np.asarray(x, np.float32).astype(ml_dtypes.bfloat16).astype(np.float64), axis, -1)
    blocks = v.reshape(v.shape[:-1] + (-1, 32))
    amax = np.abs(blocks).max(-1, keepdims=True)
    byte = np.maximum(np.where(amax > 0, np.frexp(amax)[1] - 1 + 127, 0) - down, 1)
    scale = np.exp2(byte - 127.0)
    codes = (blocks / scale).astype(np.float32).astype(dtype).astype(np.float64)
    return np.moveaxis((codes * scale).reshape(v.shape), -1, axis)


WIDE = False


def mx_kscale(k):
    if not WIDE:
        return np.ones(k)
    levels = np.array([10, -10, 5, -5, 0])
    if k % 512:
        return np.exp2(np.random.permutation(np.resize(levels, k // 32))).repeat(32)
    a = np.empty((k // 512, 16))
    for p in range(k // 512):
        a[p, :8] = np.random.permutation(np.resize(levels, 8))
        for g in range(8):
            far = levels[np.abs(levels - a[p, g]) >= 10]
            a[p, g + 8] = far[np.random.randint(len(far))]
    return np.exp2(a.ravel()).repeat(32)


def f64(x):
    return np.asarray(x).astype(np.float64)


def striped(idx):
    return np.tile(idx.reshape(-1, 16).T, (8, 1)).astype(np.uint16)


def unstriped(offs):
    return offs[:16].T.reshape(-1).astype(np.int64)


E2M1 = np.array([0.0, 0.5, 1.0, 1.5, 2.0, 3.0, 4.0, 6.0, -0.0, -0.5, -1.0, -1.5, -2.0, -3.0, -4.0, -6.0])


def pack_weight(w, fmt):
    k, n = w.shape
    w = f64(np.asarray(w, np.float32).astype(ml_dtypes.bfloat16)).reshape(k // 32, 32, n)
    amax = np.abs(w).max(1)
    if fmt == "e4m3":
        byte = np.frexp(amax)[1] - 1 + 127 - 7
    else:
        mant, ex = np.frexp(amax / 6.0)
        byte = np.where(mant > 0.5, ex, ex - 1) + 127
    byte = np.clip(np.where(amax > 0, byte, 1), 1, 254)
    scaled = (w * np.exp2(127.0 - byte)[:, None, :]).reshape(k, n).astype(np.float32)
    by_word = np.ascontiguousarray(scaled.reshape(k // 512, 128, 4, n).transpose(0, 1, 3, 2))
    if fmt == "e4m3":
        words = by_word.astype(ml_dtypes.float8_e4m3fn).view(np.uint8)
    else:
        c = by_word.astype(ml_dtypes.float4_e2m1fn).view(np.uint8) & 0xF
        words = (c[..., 0::2] | (c[..., 1::2] << 4)).reshape(k // 512, 128, 2 * n)
    return np.ascontiguousarray(words), np.ascontiguousarray(byte.astype(np.uint8).reshape(k // 512, 16, n))


def unpack_weight(words, scales, fmt):
    g, _, n = scales.shape
    words = np.ascontiguousarray(words).reshape(g, 128, n, -1)
    if fmt == "e4m3":
        vals = words.view(ml_dtypes.float8_e4m3fn).astype(np.float64)
    else:
        nib = np.empty((g, 128, n, 4), np.uint8)
        nib[..., 0::2] = words & 0xF
        nib[..., 1::2] = words >> 4
        vals = E2M1[nib]
    vals = vals * np.repeat(np.exp2(scales.astype(np.float64) - 127.0), 8, axis=1)[..., None]
    return vals.transpose(0, 1, 3, 2).reshape(g * 512, n)


def gelu(v):
    return 0.5 * v * (1.0 + np.tanh(np.sqrt(2.0 / np.pi) * (v + 0.044715 * v**3)))


K, T, E, C, N = 1024, 1536, 12, 256, 128
K8 = 512


def by_expert(wq, xq):
    return np.concatenate([wq[e].T @ xq[:, e * C:(e + 1) * C] for e in range(E)], axis=1)


def setup_inputs():
    n = np.random.standard_normal
    s = mx_kscale(K)[:, None]
    first = np.random.permutation(np.repeat(np.arange(E), T // E))
    second = (first + 1 + np.random.permutation(np.repeat(np.arange(E - 1), -(-T // (E - 1)))[:T])) % E
    while np.bincount(second, minlength=E).max() != T // E:
        load = np.bincount(second, minlength=E); hi, lo = int(load.argmax()), int(load.argmin())
        t = np.flatnonzero((second == hi) & (first != lo))[0]; second[t] = lo
    slot_token = np.empty(E * C, np.int64); pos = np.empty((2, T), np.int64); fill = np.zeros(E, np.int64)
    place = np.stack([np.random.permutation(C) for _ in range(E)])
    for r, deal in enumerate((first, second)):
        for t in np.random.permutation(T):
            e = deal[t]; j = e * C + place[e, fill[e]]; fill[e] += 1; slot_token[j] = t; pos[r, t] = j
    g = np.random.uniform(0.2, 0.8, T)
    w = n((E, K, N)) / np.sqrt(K) / s[None]
    w8 = [pack_weight(m[:K8], "e4m3") for m in w]
    w4 = [pack_weight(m[K8:], "e2m1") for m in w]
    return {
        "xT": (n((K, T)) * s).astype(np.float32),
        "w8_words": np.stack([m[0] for m in w8]),
        "w8_scales": np.stack([m[1] for m in w8]),
        "w4_words": np.stack([m[0] for m in w4]),
        "w4_scales": np.stack([m[1] for m in w4]),
        "b": (0.3 * n((N, E))).astype(np.float32),
        "gate": np.stack([np.tile(g, (N, 1)), np.tile(1.0 - g, (N, 1))]).astype(np.float32),
        "offs": striped(slot_token),
        "pos1": striped(pos[0]),
        "pos2": striped(pos[1]),
    }


def reference(xT, w8_words, w8_scales, w4_words, w4_scales, b, gate, offs, pos1, pos2):
    idx = unstriped(offs)
    w = np.stack([np.concatenate([unpack_weight(w8_words[e], w8_scales[e], "e4m3"), unpack_weight(w4_words[e], w4_scales[e], "e2m1")]) for e in range(E)])
    xq = mxq(f64(xT)[:, idx], 0, "e4m3")
    y = by_expert(w, xq)
    y = gelu(y + np.repeat(f64(b), C, axis=1))
    return f64(gate[0]) * y[:, unstriped(pos1)] + f64(gate[1]) * y[:, unstriped(pos2)]

@@ -1,0 +1,188 @@
+from contextlib import ExitStack
+
+import concourse.mybir as mybir
+
+K, T, E, C, N = 1024, 1536, 12, 256, 128
+S = E * C
+FLOPS = 2 * S * K * N
+
+P = 128
+PACK = 4
+K_PASS = P * PACK
+GROUP = 128
+
+F32 = mybir.dt.float32
+BF16 = mybir.dt.bfloat16
+I32 = mybir.dt.int32
+U32 = mybir.dt.uint32
+U16 = mybir.dt.uint16
+U8 = mybir.dt.uint8
+FP8X4 = mybir.dt.float8_e4m3fn_x4
+FP4X4 = mybir.dt.float4_e2m1fn_x4
+ACT = mybir.ActivationFunctionType
+MULT, ADD = mybir.AluOpType.mult, mybir.AluOpType.add
+
+CHUNKS = (
+    ((0, 512, 256), (512, 512, 256), (1024, 256, 160), (1280, 256, 160)),
+    ((0, 512, 0), (512, 512, 0), (1024, 256, 0), (1280, 256, 128)),
+)
+SCALE_ROW = (4, 0)
+
+
+def tile_moe_pln_lin_gelu_kernel(
+    tc, xT, w8_words, w8_scales, w4_words, w4_scales, b, gate, offs, pos1, pos2, out
+):
+    nc = tc.nc
+    with ExitStack() as ctx:
+        lists = ctx.enter_context(tc.tile_pool(name="lists", bufs=1))
+        keep = ctx.enter_context(tc.tile_pool(name="keep", bufs=1))
+        psum = ctx.enter_context(tc.psum_pool(name="psum", bufs=1))
+
+        offs_sb = lists.tile([P, S // 16], U16, name="offs_sb")
+        pos1_sb = lists.tile([P, T // 16], U16, name="pos1_sb")
+        pos2_sb = lists.tile([P, T // 16], U16, name="pos2_sb")
+
+        x_words = [keep.tile([P, T], U32, name=f"x_words{a}", align_bytes=64) for a in range(2)]
+        x_scales = keep.tile([P, T], U8, name="x_scales", align_bytes=64)
+        slot_words = [keep.tile([P, S], U32, name=f"slot_words{a}", align_bytes=64) for a in range(2)]
+        slot_scales = keep.tile([P, S], U8, name="slot_scales", align_bytes=64)
+        w8_sb = keep.tile([P, E * N * 4], U8, name="w8_sb", align_bytes=64)
+        w4_sb = keep.tile([P, E * N * 2], U8, name="w4_sb", align_bytes=64)
+        w8_planes = keep.tile([P, E * N], U8, name="w8_planes", align_bytes=64)
+        w4_planes = keep.tile([P, E * N], U8, name="w4_planes", align_bytes=64)
+        bias = keep.tile([P, E], F32, name="bias")
+        gates = [keep.tile([P, T], F32, name=f"gate{r}") for r in range(2)]
+        y = keep.tile([P, S], F32, name="y")
+        warm = keep.tile([P, 1], F32, name="warm")
+
+        nc.gpsimd.memset(x_scales[:], 0)
+        nc.vector.memset(warm[:], 0.0)
+        nc.vector.memset(w8_planes[:].bitcast(I32), 0)
+        nc.vector.memset(w4_planes[:].bitcast(I32), 0)
+        nc.scalar.activation(warm[:], warm[:], ACT.Gelu_apprx_tanh)
+
+        raw = {}
+
+        def load_chunk(a, c):
+            t0, width, _ = CHUNKS[a][c]
+            tile = keep.tile([P, PACK, width], F32, name=f"raw{a}_{c}")
+            rows = xT[a * K_PASS : (a + 1) * K_PASS, t0 : t0 + width]
+            nc.sync.dma_start(out=tile[:], in_=rows.rearrange("(p j) w -> p j w", j=PACK))
+            raw[a, c] = tile
+
+        load_chunk(0, 0)
+        nc.sync.dma_start(offs_sb[:], offs)
+        for c in (1, 2, 3):
+            load_chunk(0, c)
+        for c in range(4):
+            load_chunk(1, c)
+
+        for planes, scales in ((w8_planes, w8_scales), (w4_planes, w4_scales)):
+            for q in range(4):
+                nc.sync.dma_start(
+                    out=planes[32 * q : 32 * q + 4, :].bitcast(I32).rearrange("q (e n) -> q e n", e=E),
+                    in_=scales[:, 0, 4 * q : 4 * q + 4, :].bitcast(I32).rearrange("e q n -> q e n"),
+                )
+        nc.sync.dma_start(bias[:], b)
+        half = E // 2
+        for h in range(2):
+            experts = slice(h * half, (h + 1) * half)
+            nc.sync.dma_start(
+                out=w8_sb[:, h * half * N * 4 : (h + 1) * half * N * 4].bitcast(I32).rearrange("p (e n) -> p e n", e=half),
+                in_=w8_words[experts, 0].rearrange("e p n r -> e p (n r)").bitcast(I32).rearrange("e p n -> p e n"),
+            )
+            nc.sync.dma_start(
+                out=w4_sb[:, h * half * N * 2 : (h + 1) * half * N * 2].bitcast(I32).rearrange("p (e n) -> p e n", e=half),
+                in_=w4_words[experts, 0].bitcast(I32).rearrange("e p n -> p e n"),
+            )
+        nc.sync.dma_start(pos1_sb[:], pos1)
+        nc.sync.dma_start(pos2_sb[:], pos2)
+        for r in range(2):
+            nc.sync.dma_start(gates[r][:], gate[r])
+
+        grouped = {}
+
+        def interleave(a, c):
+            _, width, by_vector = CHUNKS[a][c]
+            tile = keep.tile([P, width, PACK], BF16, name=f"grouped{a}_{c}", align_bytes=64)
+            grouped[a, c] = tile
+
+            def views(lo, hi):
+                dst = tile[:, lo:hi, :].rearrange("p (c i) t -> p c t i", i=4)
+                src = raw[a, c][:, :, lo:hi].rearrange("p t (c i) -> p c t i", i=4)
+                return dst, src
+
+            if by_vector < width:
+                dst, src = views(by_vector, width)
+                nc.scalar.activation(dst, src, ACT.Copy)
+            if by_vector > 0:
+                dst, src = views(0, by_vector)
+                nc.vector.tensor_copy(dst, src)
+
+        def quantise(a, c):
+            t0, width, _ = CHUNKS[a][c]
+            nc.vector.quantize_mx(
+                out=x_words[a][:, t0 : t0 + width].bitcast(FP8X4),
+                scales=x_scales[SCALE_ROW[a] : P, t0 : t0 + width],
+                in_=grouped[a, c][:].rearrange("p w j -> p (w j)"),
+            )
+
+        def gather(dst, window, lo, hi):
+            nc.vector.tensor_copy(dst[:, lo:hi], window[:].indirect(offs_sb[:, lo // 16 : hi // 16]))
+
+        for c in range(4):
+            interleave(0, c)
+            quantise(0, c)
+        for c in range(3):
+            interleave(1, c)
+        gather(slot_words[0], x_words[0], 0, 1024)
+        gather(slot_words[0], x_words[0], 1024, 2048)
+        quantise(1, 0)
+        gather(slot_words[0], x_words[0], 2048, 3072)
+        quantise(1, 1)
+        interleave(1, 3)
+        quantise(1, 2)
+        quantise(1, 3)
+
+        def expert(e):
+            bank = psum.tile([P, C], F32, name=f"bank{e % 8}")
+            for g in range(C // GROUP):
+                cols = slice(e * C + g * GROUP, e * C + (g + 1) * GROUP)
+                nc.tensor.matmul_mx(
+                    out=bank[:, g * GROUP : (g + 1) * GROUP],
+                    lhsT=w8_sb[:, e * N * 4 : (e + 1) * N * 4].bitcast(FP8X4),
+                    lhsT_scale=w8_planes[:, e * N : (e + 1) * N],
+                    rhs=slot_words[0][:, cols].bitcast(FP8X4),
+                    rhs_scale=slot_scales[SCALE_ROW[0] : P, cols],
+                    start=True,
+                    stop=False,
+                )
+                nc.tensor.matmul_mx(
+                    out=bank[:, g * GROUP : (g + 1) * GROUP],
+                    lhsT=w4_sb[:, e * N * 2 : (e + 1) * N * 2].bitcast(FP4X4),
+                    lhsT_scale=w4_planes[:, e * N : (e + 1) * N],
+                    rhs=slot_words[1][:, cols].bitcast(FP8X4),
+                    rhs_scale=slot_scales[SCALE_ROW[1] : P, cols],
+                    start=False,
+                    stop=True,
+                )
+            nc.scalar.activation(y[:, e * C : (e + 1) * C], bank[:], ACT.Gelu_apprx_tanh, bias=bias[:, e : e + 1])
+
+        for lo, hi in ((0, 512), (512, 1024), (1024, 1536), (1536, 2048), (2048, 2560), (2560, 2816), (2816, 3072)):
+            gather(slot_scales, x_scales, lo, hi)
+            gather(slot_words[1], x_words[1], lo, hi)
+            for e in range(lo // C, hi // C):
+                expert(e)
+
+        pieces = ((0, 640), (640, 1280), (1280, 1536))
+        picked = {}
+        for lo, hi in pieces:
+            for r, pos in ((0, pos1_sb), (1, pos2_sb)):
+                tile = keep.tile([P, hi - lo], F32, name=f"picked{r}_{lo}")
+                nc.vector.tensor_tensor(
+                    tile[:], y[:].indirect(pos[:, lo // 16 : hi // 16]), gates[r][:, lo:hi], MULT
+                )
+                picked[r] = tile
+            total = keep.tile([P, hi - lo], F32, name=f"total_{lo}")
+            nc.vector.tensor_tensor(total[:], picked[0][:], picked[1][:], ADD)
+            nc.sync.dma_start(out[:, lo:hi], total[:])

@@ -23,7 +23,7 @@ ACT = mybir.ActivationFunctionType
 MULT, ADD = mybir.AluOpType.mult, mybir.AluOpType.add
 
 CHUNKS = (
-    ((0, 512, 256), (512, 512, 256), (1024, 256, 160), (1280, 256, 160)),
+    ((0, 512, 256), (512, 512, 256), (1024, 256, 160), (1280, 256, 192)),
     ((0, 512, 0), (512, 512, 0), (1024, 256, 0), (1280, 256, 128)),
 )
 SCALE_ROW = (4, 0)
@@ -137,52 +137,96 @@ def tile_moe_pln_lin_gelu_kernel(
             interleave(1, c)
         gather(slot_words[0], x_words[0], 0, 1024)
         gather(slot_words[0], x_words[0], 1024, 2048)
-        quantise(1, 0)
         gather(slot_words[0], x_words[0], 2048, 3072)
+        quantise(1, 0)
         quantise(1, 1)
         interleave(1, 3)
         quantise(1, 2)
         quantise(1, 3)
 
+        banks = {}
+
+        def first_pass(e, g):
+            bank = banks[e, g]
+            cols = slice(e * C + g * GROUP, e * C + (g + 1) * GROUP)
+            nc.tensor.matmul_mx(
+                out=bank,
+                lhsT=w8_sb[:, e * N * 4 : (e + 1) * N * 4].bitcast(FP8X4),
+                lhsT_scale=w8_planes[:, e * N : (e + 1) * N],
+                rhs=slot_words[0][:, cols].bitcast(FP8X4),
+                rhs_scale=slot_scales[SCALE_ROW[0] : P, cols],
+                start=True,
+                stop=False,
+            )
+
+        def second_pass(e, g):
+            bank = banks[e, g]
+            cols = slice(e * C + g * GROUP, e * C + (g + 1) * GROUP)
+            nc.tensor.matmul_mx(
+                out=bank,
+                lhsT=w4_sb[:, e * N * 2 : (e + 1) * N * 2].bitcast(FP4X4),
+                lhsT_scale=w4_planes[:, e * N : (e + 1) * N],
+                rhs=slot_words[1][:, cols].bitcast(FP8X4),
+                rhs_scale=slot_scales[SCALE_ROW[1] : P, cols],
+                start=False,
+                stop=True,
+            )
+
+        def gelu(e, bank, lo, hi):
+            nc.scalar.activation(y[:, lo:hi], bank, ACT.Gelu_apprx_tanh, bias=bias[:, e : e + 1])
+
+        last = E - 1
+        tail_banks = [psum.tile([P, GROUP], F32, name=f"tail{g}") for g in range(2)]
+        for g in range(2):
+            banks[last, g] = tail_banks[g][:]
+
         def expert(e):
-            bank = psum.tile([P, C], F32, name=f"bank{e % 8}")
-            for g in range(C // GROUP):
-                cols = slice(e * C + g * GROUP, e * C + (g + 1) * GROUP)
-                nc.tensor.matmul_mx(
-                    out=bank[:, g * GROUP : (g + 1) * GROUP],
-                    lhsT=w8_sb[:, e * N * 4 : (e + 1) * N * 4].bitcast(FP8X4),
-                    lhsT_scale=w8_planes[:, e * N : (e + 1) * N],
-                    rhs=slot_words[0][:, cols].bitcast(FP8X4),
-                    rhs_scale=slot_scales[SCALE_ROW[0] : P, cols],
-                    start=True,
-                    stop=False,
-                )
-                nc.tensor.matmul_mx(
-                    out=bank[:, g * GROUP : (g + 1) * GROUP],
-                    lhsT=w4_sb[:, e * N * 2 : (e + 1) * N * 2].bitcast(FP4X4),
-                    lhsT_scale=w4_planes[:, e * N : (e + 1) * N],
-                    rhs=slot_words[1][:, cols].bitcast(FP8X4),
-                    rhs_scale=slot_scales[SCALE_ROW[1] : P, cols],
-                    start=False,
-                    stop=True,
-                )
-            nc.scalar.activation(y[:, e * C : (e + 1) * C], bank[:], ACT.Gelu_apprx_tanh, bias=bias[:, e : e + 1])
+            bank = psum.tile([P, C], F32, name=f"bank{e % 6}")
+            for g in range(2):
+                banks[e, g] = bank[:, g * GROUP : (g + 1) * GROUP]
+                first_pass(e, g)
+                second_pass(e, g)
+            gelu(e, bank[:], e * C, (e + 1) * C)
 
-        for lo, hi in ((0, 512), (512, 1024), (1024, 1536), (1536, 2048), (2048, 2560), (2560, 2816), (2816, 3072)):
-            gather(slot_scales, x_scales, lo, hi)
-            gather(slot_words[1], x_words[1], lo, hi)
-            for e in range(lo // C, hi // C):
-                expert(e)
+        for lo in range(0, S, 1024):
+            gather(slot_scales, x_scales, lo, lo + 1024)
+            if lo == 2048:
+                for g in range(2):
+                    first_pass(last, g)
+                cuts = (2048, 2560, 2816)
+            else:
+                cuts = (lo, lo + 512, lo + 1024)
+            for a0, a1 in zip(cuts[:-1], cuts[1:]):
+                gather(slot_words[1], x_words[1], a0, a1)
+                for e in range(a0 // C, a1 // C):
+                    expert(e)
+        gather(slot_words[1], x_words[1], 2816, 3072)
+        for g in range(2):
+            second_pass(last, g)
+            gelu(last, banks[last, g], last * C + g * GROUP, last * C + (g + 1) * GROUP)
 
-        pieces = ((0, 640), (640, 1280), (1280, 1536))
+        pieces = ((0, 640), (640, 1344), (1344, 1536))
         picked = {}
-        for lo, hi in pieces:
-            for r, pos in ((0, pos1_sb), (1, pos2_sb)):
-                tile = keep.tile([P, hi - lo], F32, name=f"picked{r}_{lo}")
-                nc.vector.tensor_tensor(
-                    tile[:], y[:].indirect(pos[:, lo // 16 : hi // 16]), gates[r][:, lo:hi], MULT
-                )
-                picked[r] = tile
-            total = keep.tile([P, hi - lo], F32, name=f"total_{lo}")
-            nc.vector.tensor_tensor(total[:], picked[0][:], picked[1][:], ADD)
+
+        def pick(r, i):
+            lo, hi = pieces[i]
+            pos = (pos1_sb, pos2_sb)[r]
+            tile = keep.tile([P, hi - lo], F32, name=f"picked{r}_{i}")
+            nc.vector.tensor_tensor(tile[:], y[:].indirect(pos[:, lo // 16 : hi // 16]), gates[r][:, lo:hi], MULT)
+            picked[r, i] = tile
+
+        def combine(i):
+            lo, hi = pieces[i]
+            total = keep.tile([P, hi - lo], F32, name=f"total{i}")
+            nc.vector.tensor_tensor(total[:], picked[0, i][:], picked[1, i][:], ADD)
             nc.sync.dma_start(out[:, lo:hi], total[:])
+
+        pick(0, 0)
+        pick(1, 0)
+        pick(0, 1)
+        combine(0)
+        pick(1, 1)
+        pick(0, 2)
+        combine(1)
+        pick(1, 2)
+        combine(2)

@@ -23,7 +23,7 @@ ACT = mybir.ActivationFunctionType
 MULT, ADD = mybir.AluOpType.mult, mybir.AluOpType.add
 
 CHUNKS = (
-    ((0, 512, 256), (512, 512, 256), (1024, 256, 160), (1280, 256, 192)),
+    ((0, 768, 512), (768, 512, 320), (1280, 256, 192)),
     ((0, 512, 0), (512, 512, 0), (1024, 256, 0), (1280, 256, 128)),
 )
 SCALE_ROW = (4, 0)
@@ -72,7 +72,7 @@ def tile_moe_pln_lin_gelu_kernel(
 
         load_chunk(0, 0)
         nc.sync.dma_start(offs_sb[:], offs)
-        for c in (1, 2, 3):
+        for c in (1, 2):
             load_chunk(0, c)
         for c in range(4):
             load_chunk(1, c)
@@ -121,16 +121,18 @@ def tile_moe_pln_lin_gelu_kernel(
 
         def quantise(a, c):
             t0, width, _ = CHUNKS[a][c]
-            nc.vector.quantize_mx(
-                out=x_words[a][:, t0 : t0 + width].bitcast(FP8X4),
-                scales=x_scales[SCALE_ROW[a] : P, t0 : t0 + width],
-                in_=grouped[a, c][:].rearrange("p w j -> p (w j)"),
-            )
+            for lo in range(0, width, 512):
+                hi = min(width, lo + 512)
+                nc.vector.quantize_mx(
+                    out=x_words[a][:, t0 + lo : t0 + hi].bitcast(FP8X4),
+                    scales=x_scales[SCALE_ROW[a] : P, t0 + lo : t0 + hi],
+                    in_=grouped[a, c][:, lo:hi, :].rearrange("p w j -> p (w j)"),
+                )
 
         def gather(dst, window, lo, hi):
             nc.vector.tensor_copy(dst[:, lo:hi], window[:].indirect(offs_sb[:, lo // 16 : hi // 16]))
 
-        for c in range(4):
+        for c in range(3):
             interleave(0, c)
             quantise(0, c)
         for c in range(3):
@@ -195,7 +197,7 @@ def tile_moe_pln_lin_gelu_kernel(
                     first_pass(last, g)
                 cuts = (2048, 2560, 2816)
             else:
-                cuts = (lo, lo + 512, lo + 1024)
+                cuts = (lo, lo + 1024)
             for a0, a1 in zip(cuts[:-1], cuts[1:]):
                 gather(slot_words[1], x_words[1], a0, a1)
                 for e in range(a0 // C, a1 // C):

@@ -70,10 +70,9 @@ def tile_moe_pln_lin_gelu_kernel(
             nc.sync.dma_start(out=tile[:], in_=rows.rearrange("(p j) w -> p j w", j=PACK))
             raw[a, c] = tile
 
-        load_chunk(0, 0)
-        nc.sync.dma_start(offs_sb[:], offs)
-        for c in (1, 2):
+        for c in range(3):
             load_chunk(0, c)
+        nc.sync.dma_start(offs_sb[:], offs)
         for c in range(4):
             load_chunk(1, c)
 
@@ -207,7 +206,7 @@ def tile_moe_pln_lin_gelu_kernel(
             second_pass(last, g)
             gelu(last, banks[last, g], last * C + g * GROUP, last * C + (g + 1) * GROUP)
 
-        pieces = ((0, 640), (640, 1344), (1344, 1536))
+        pieces = ((0, 704), (704, 1408), (1408, 1536))
         picked = {}
 
         def pick(r, i):

@@ -23,8 +23,8 @@ ACT = mybir.ActivationFunctionType
 MULT, ADD = mybir.AluOpType.mult, mybir.AluOpType.add
 
 CHUNKS = (
-    ((0, 768, 512), (768, 512, 320), (1280, 256, 192)),
-    ((0, 512, 0), (512, 512, 0), (1024, 256, 0), (1280, 256, 128)),
+    ((0, 768, 384), (768, 512, 256), (1280, 256, 160)),
+    ((0, 256, 0), (256, 512, 0), (768, 512, 0), (1280, 256, 128)),
 )
 SCALE_ROW = (4, 0)
 

from contextlib import ExitStack

import concourse.mybir as mybir

K, T, E, C, N = 1024, 1536, 12, 256, 128
S = E * C
FLOPS = 2 * S * K * N

P = 128
PACK = 4
K_PASS = P * PACK
GROUP = 128

F32 = mybir.dt.float32
BF16 = mybir.dt.bfloat16
I32 = mybir.dt.int32
U32 = mybir.dt.uint32
U16 = mybir.dt.uint16
U8 = mybir.dt.uint8
FP8X4 = mybir.dt.float8_e4m3fn_x4
FP4X4 = mybir.dt.float4_e2m1fn_x4
ACT = mybir.ActivationFunctionType
MULT, ADD = mybir.AluOpType.mult, mybir.AluOpType.add

CHUNKS = (
    ((0, 768, 384), (768, 512, 256), (1280, 256, 160)),
    ((0, 256, 0), (256, 512, 0), (768, 512, 0), (1280, 256, 128)),
)
SCALE_ROW = (4, 0)


def tile_moe_pln_lin_gelu_kernel(
    tc, xT, w8_words, w8_scales, w4_words, w4_scales, b, gate, offs, pos1, pos2, out
):
    nc = tc.nc
    with ExitStack() as ctx:
        lists = ctx.enter_context(tc.tile_pool(name="lists", bufs=1))
        keep = ctx.enter_context(tc.tile_pool(name="keep", bufs=1))
        psum = ctx.enter_context(tc.psum_pool(name="psum", bufs=1))

        offs_sb = lists.tile([P, S // 16], U16, name="offs_sb")
        pos1_sb = lists.tile([P, T // 16], U16, name="pos1_sb")
        pos2_sb = lists.tile([P, T // 16], U16, name="pos2_sb")

        x_words = [keep.tile([P, T], U32, name=f"x_words{a}", align_bytes=64) for a in range(2)]
        x_scales = keep.tile([P, T], U8, name="x_scales", align_bytes=64)
        slot_words = [keep.tile([P, S], U32, name=f"slot_words{a}", align_bytes=64) for a in range(2)]
        slot_scales = keep.tile([P, S], U8, name="slot_scales", align_bytes=64)
        w8_sb = keep.tile([P, E * N * 4], U8, name="w8_sb", align_bytes=64)
        w4_sb = keep.tile([P, E * N * 2], U8, name="w4_sb", align_bytes=64)
        w8_planes = keep.tile([P, E * N], U8, name="w8_planes", align_bytes=64)
        w4_planes = keep.tile([P, E * N], U8, name="w4_planes", align_bytes=64)
        bias = keep.tile([P, E], F32, name="bias")
        gates = [keep.tile([P, T], F32, name=f"gate{r}") for r in range(2)]
        y = keep.tile([P, S], F32, name="y")
        warm = keep.tile([P, 1], F32, name="warm")

        nc.gpsimd.memset(x_scales[:], 0)
        nc.vector.memset(warm[:], 0.0)
        nc.vector.memset(w8_planes[:].bitcast(I32), 0)
        nc.vector.memset(w4_planes[:].bitcast(I32), 0)
        nc.scalar.activation(warm[:], warm[:], ACT.Gelu_apprx_tanh)

        raw = {}

        def load_chunk(a, c):
            t0, width, _ = CHUNKS[a][c]
            tile = keep.tile([P, PACK, width], F32, name=f"raw{a}_{c}")
            rows = xT[a * K_PASS : (a + 1) * K_PASS, t0 : t0 + width]
            nc.sync.dma_start(out=tile[:], in_=rows.rearrange("(p j) w -> p j w", j=PACK))
            raw[a, c] = tile

        for c in range(3):
            load_chunk(0, c)
        nc.sync.dma_start(offs_sb[:], offs)
        for c in range(4):
            load_chunk(1, c)

        for planes, scales in ((w8_planes, w8_scales), (w4_planes, w4_scales)):
            for q in range(4):
                nc.sync.dma_start(
                    out=planes[32 * q : 32 * q + 4, :].bitcast(I32).rearrange("q (e n) -> q e n", e=E),
                    in_=scales[:, 0, 4 * q : 4 * q + 4, :].bitcast(I32).rearrange("e q n -> q e n"),
                )
        nc.sync.dma_start(bias[:], b)
        half = E // 2
        for h in range(2):
            experts = slice(h * half, (h + 1) * half)
            nc.sync.dma_start(
                out=w8_sb[:, h * half * N * 4 : (h + 1) * half * N * 4].bitcast(I32).rearrange("p (e n) -> p e n", e=half),
                in_=w8_words[experts, 0].rearrange("e p n r -> e p (n r)").bitcast(I32).rearrange("e p n -> p e n"),
            )
            nc.sync.dma_start(
                out=w4_sb[:, h * half * N * 2 : (h + 1) * half * N * 2].bitcast(I32).rearrange("p (e n) -> p e n", e=half),
                in_=w4_words[experts, 0].bitcast(I32).rearrange("e p n -> p e n"),
            )
        nc.sync.dma_start(pos1_sb[:], pos1)
        nc.sync.dma_start(pos2_sb[:], pos2)
        for r in range(2):
            nc.sync.dma_start(gates[r][:], gate[r])

        grouped = {}

        def interleave(a, c):
            _, width, by_vector = CHUNKS[a][c]
            tile = keep.tile([P, width, PACK], BF16, name=f"grouped{a}_{c}", align_bytes=64)
            grouped[a, c] = tile

            def views(lo, hi):
                dst = tile[:, lo:hi, :].rearrange("p (c i) t -> p c t i", i=4)
                src = raw[a, c][:, :, lo:hi].rearrange("p t (c i) -> p c t i", i=4)
                return dst, src

            if by_vector < width:
                dst, src = views(by_vector, width)
                nc.scalar.activation(dst, src, ACT.Copy)
            if by_vector > 0:
                dst, src = views(0, by_vector)
                nc.vector.tensor_copy(dst, src)

        def quantise(a, c):
            t0, width, _ = CHUNKS[a][c]
            for lo in range(0, width, 512):
                hi = min(width, lo + 512)
                nc.vector.quantize_mx(
                    out=x_words[a][:, t0 + lo : t0 + hi].bitcast(FP8X4),
                    scales=x_scales[SCALE_ROW[a] : P, t0 + lo : t0 + hi],
                    in_=grouped[a, c][:, lo:hi, :].rearrange("p w j -> p (w j)"),
                )

        def gather(dst, window, lo, hi):
            nc.vector.tensor_copy(dst[:, lo:hi], window[:].indirect(offs_sb[:, lo // 16 : hi // 16]))

        for c in range(3):
            interleave(0, c)
            quantise(0, c)
        for c in range(3):
            interleave(1, c)
        gather(slot_words[0], x_words[0], 0, 1024)
        gather(slot_words[0], x_words[0], 1024, 2048)
        gather(slot_words[0], x_words[0], 2048, 3072)
        quantise(1, 0)
        quantise(1, 1)
        interleave(1, 3)
        quantise(1, 2)
        quantise(1, 3)

        banks = {}

        def first_pass(e, g):
            bank = banks[e, g]
            cols = slice(e * C + g * GROUP, e * C + (g + 1) * GROUP)
            nc.tensor.matmul_mx(
                out=bank,
                lhsT=w8_sb[:, e * N * 4 : (e + 1) * N * 4].bitcast(FP8X4),
                lhsT_scale=w8_planes[:, e * N : (e + 1) * N],
                rhs=slot_words[0][:, cols].bitcast(FP8X4),
                rhs_scale=slot_scales[SCALE_ROW[0] : P, cols],
                start=True,
                stop=False,
            )

        def second_pass(e, g):
            bank = banks[e, g]
            cols = slice(e * C + g * GROUP, e * C + (g + 1) * GROUP)
            nc.tensor.matmul_mx(
                out=bank,
                lhsT=w4_sb[:, e * N * 2 : (e + 1) * N * 2].bitcast(FP4X4),
                lhsT_scale=w4_planes[:, e * N : (e + 1) * N],
                rhs=slot_words[1][:, cols].bitcast(FP8X4),
                rhs_scale=slot_scales[SCALE_ROW[1] : P, cols],
                start=False,
                stop=True,
            )

        def gelu(e, bank, lo, hi):
            nc.scalar.activation(y[:, lo:hi], bank, ACT.Gelu_apprx_tanh, bias=bias[:, e : e + 1])

        last = E - 1
        tail_banks = [psum.tile([P, GROUP], F32, name=f"tail{g}") for g in range(2)]
        for g in range(2):
            banks[last, g] = tail_banks[g][:]

        def expert(e):
            bank = psum.tile([P, C], F32, name=f"bank{e % 6}")
            for g in range(2):
                banks[e, g] = bank[:, g * GROUP : (g + 1) * GROUP]
                first_pass(e, g)
                second_pass(e, g)
            gelu(e, bank[:], e * C, (e + 1) * C)

        for lo in range(0, S, 1024):
            gather(slot_scales, x_scales, lo, lo + 1024)
            if lo == 2048:
                for g in range(2):
                    first_pass(last, g)
                cuts = (2048, 2560, 2816)
            else:
                cuts = (lo, lo + 1024)
            for a0, a1 in zip(cuts[:-1], cuts[1:]):
                gather(slot_words[1], x_words[1], a0, a1)
                for e in range(a0 // C, a1 // C):
                    expert(e)
        gather(slot_words[1], x_words[1], 2816, 3072)
        for g in range(2):
            second_pass(last, g)
            gelu(last, banks[last, g], last * C + g * GROUP, last * C + (g + 1) * GROUP)

        pieces = ((0, 704), (704, 1408), (1408, 1536))
        picked = {}

        def pick(r, i):
            lo, hi = pieces[i]
            pos = (pos1_sb, pos2_sb)[r]
            tile = keep.tile([P, hi - lo], F32, name=f"picked{r}_{i}")
            nc.vector.tensor_tensor(tile[:], y[:].indirect(pos[:, lo // 16 : hi // 16]), gates[r][:, lo:hi], MULT)
            picked[r, i] = tile

        def combine(i):
            lo, hi = pieces[i]
            total = keep.tile([P, hi - lo], F32, name=f"total{i}")
            nc.vector.tensor_tensor(total[:], picked[0, i][:], picked[1, i][:], ADD)
            nc.sync.dma_start(out[:, lo:hi], total[:])

        pick(0, 0)
        pick(1, 0)
        pick(0, 1)
        combine(0)
        pick(1, 1)
        pick(0, 2)
        combine(1)
        pick(1, 2)
        combine(2)
